import numpy as np
import ml_dtypes


def mxq(x, axis, fmt="e4m3"):
    dtype, down = {"e4m3": (ml_dtypes.float8_e4m3fn, 7), "e5m2": (ml_dtypes.float8_e5m2, 14)}[fmt]
    v = np.moveaxis(np.asarray(x, np.float32).astype(ml_dtypes.bfloat16).astype(np.float64), axis, -1)
    blocks = v.reshape(v.shape[:-1] + (-1, 32))
    amax = np.abs(blocks).max(-1, keepdims=True)
    byte = np.maximum(np.where(amax > 0, np.frexp(amax)[1] - 1 + 127, 0) - down, 1)
    scale = np.exp2(byte - 127.0)
    codes = (blocks / scale).astype(np.float32).astype(dtype).astype(np.float64)
    return np.moveaxis((codes * scale).reshape(v.shape), -1, axis)


WIDE = False


def mx_kscale(k):
    if not WIDE:
        return np.ones(k)
    levels = np.array([10, -10, 5, -5, 0])
    if k % 512:
        return np.exp2(np.random.permutation(np.resize(levels, k // 32))).repeat(32)
    a = np.empty((k // 512, 16))
    for p in range(k // 512):
        a[p, :8] = np.random.permutation(np.resize(levels, 8))
        for g in range(8):
            far = levels[np.abs(levels - a[p, g]) >= 10]
            a[p, g + 8] = far[np.random.randint(len(far))]
    return np.exp2(a.ravel()).repeat(32)


def f64(x):
    return np.asarray(x).astype(np.float64)


def striped(idx):
    return np.tile(idx.reshape(-1, 16).T, (8, 1)).astype(np.uint16)


def unstriped(offs):
    return offs[:16].T.reshape(-1).astype(np.int64)


E2M1 = np.array([0.0, 0.5, 1.0, 1.5, 2.0, 3.0, 4.0, 6.0, -0.0, -0.5, -1.0, -1.5, -2.0, -3.0, -4.0, -6.0])


def pack_weight(w, fmt):
    k, n = w.shape
    w = f64(np.asarray(w, np.float32).astype(ml_dtypes.bfloat16)).reshape(k // 32, 32, n)
    amax = np.abs(w).max(1)
    if fmt == "e4m3":
        byte = np.frexp(amax)[1] - 1 + 127 - 7
    else:
        mant, ex = np.frexp(amax / 6.0)
        byte = np.where(mant > 0.5, ex, ex - 1) + 127
    byte = np.clip(np.where(amax > 0, byte, 1), 1, 254)
    scaled = (w * np.exp2(127.0 - byte)[:, None, :]).reshape(k, n).astype(np.float32)
    by_word = np.ascontiguousarray(scaled.reshape(k // 512, 128, 4, n).transpose(0, 1, 3, 2))
    if fmt == "e4m3":
        words = by_word.astype(ml_dtypes.float8_e4m3fn).view(np.uint8)
    else:
        c = by_word.astype(ml_dtypes.float4_e2m1fn).view(np.uint8) & 0xF
        words = (c[..., 0::2] | (c[..., 1::2] << 4)).reshape(k // 512, 128, 2 * n)
    return np.ascontiguousarray(words), np.ascontiguousarray(byte.astype(np.uint8).reshape(k // 512, 16, n))


def unpack_weight(words, scales, fmt):
    g, _, n = scales.shape
    words = np.ascontiguousarray(words).reshape(g, 128, n, -1)
    if fmt == "e4m3":
        vals = words.view(ml_dtypes.float8_e4m3fn).astype(np.float64)
    else:
        nib = np.empty((g, 128, n, 4), np.uint8)
        nib[..., 0::2] = words & 0xF
        nib[..., 1::2] = words >> 4
        vals = E2M1[nib]
    vals = vals * np.repeat(np.exp2(scales.astype(np.float64) - 127.0), 8, axis=1)[..., None]
    return vals.transpose(0, 1, 3, 2).reshape(g * 512, n)


def silu(v):
    return v / (1.0 + np.exp(-np.maximum(v, -700.0)))


K, T, E, C, N = 1536, 1024, 12, 256, 128
TOP = 3
K8 = 512


def by_expert(wq, xq):
    return np.concatenate([wq[e].T @ xq[:, e * C:(e + 1) * C] for e in range(E)], axis=1)


def setup_inputs():
    n = np.random.standard_normal
    s = mx_kscale(K)[:, None]
    deal = np.repeat(np.arange(E), C).reshape(TOP, T)[:, np.random.permutation(T)]
    deal = np.take_along_axis(deal, np.argsort(np.random.rand(TOP, T), axis=0), axis=0)
    for _ in range(8):
        s_, t_ = np.random.permutation(T).reshape(2, -1); r = np.random.randint(TOP, size=T // 2); x, y = deal[r, s_].copy(), deal[r, t_].copy()
        ok = ~((deal[:, s_] == y).any(0) | (deal[:, t_] == x).any(0)); deal[r[ok], s_[ok]] = y[ok]; deal[r[ok], t_[ok]] = x[ok]
    order = np.lexsort((np.random.rand(TOP * T), deal.reshape(-1)))
    slot_token = order % T; pos = np.empty(TOP * T, np.int64); pos[order] = np.arange(TOP * T); pos = pos.reshape(TOP, T)
    g = np.random.uniform(0.5, 1.5, (TOP, T)); g = g / g.sum(0)
    w = n((E, K, N)) / np.sqrt(K) / s[None]
    w8 = [pack_weight(m[:K8], "e4m3") for m in w]
    w4 = [pack_weight(m[K8:], "e2m1") for m in w]
    return {
        "xT": (n((K, T)) * s).astype(np.float32),
        "w8_words": np.stack([m[0] for m in w8]),
        "w8_scales": np.stack([m[1] for m in w8]),
        "w4_words": np.stack([m[0] for m in w4]),
        "w4_scales": np.stack([m[1] for m in w4]),
        "b": (0.3 * n((N, E))).astype(np.float32),
        "gate": np.stack([np.tile(r, (N, 1)) for r in g]).astype(np.float32),
        "offs": striped(slot_token),
        "pos1": striped(pos[0]),
        "pos2": striped(pos[1]),
        "pos3": striped(pos[2]),
    }


def reference(xT, w8_words, w8_scales, w4_words, w4_scales, b, gate, offs, pos1, pos2, pos3):
    idx = unstriped(offs)
    w = np.stack([np.concatenate([unpack_weight(w8_words[e], w8_scales[e], "e4m3"), unpack_weight(w4_words[e], w4_scales[e], "e2m1")]) for e in range(E)])
    xq = mxq(f64(xT)[:, idx], 0, "e4m3")
    y = by_expert(w, xq)
    y = silu(y + np.repeat(f64(b), C, axis=1))
    return sum(f64(gate[r]) * y[:, unstriped(p)] for r, p in enumerate((pos1, pos2, pos3)))

@@ -1,0 +1,192 @@
+from contextlib import ExitStack
+
+import concourse.mybir as mybir
+
+K, T, E, C, N = 1536, 1024, 12, 256, 128
+TOP = 3
+S = E * C
+PASSES = 3
+P = 128
+FLOPS = 2 * S * K * N
+
+F32 = mybir.dt.float32
+BF16 = mybir.dt.bfloat16
+I32 = mybir.dt.int32
+U32 = mybir.dt.uint32
+U16 = mybir.dt.uint16
+U8 = mybir.dt.uint8
+FP8X4 = mybir.dt.float8_e4m3fn_x4
+FP4X4 = mybir.dt.float4_e2m1fn_x4
+COPY = mybir.ActivationFunctionType.Copy
+SILU = mybir.ActivationFunctionType.Silu
+MULT = mybir.AluOpType.mult
+
+CUT = 1536
+
+
+def tile_moe_tk_lin_silu_kernel(
+    tc, xT, w8_words, w8_scales, w4_words, w4_scales, b, gate, offs, pos1, pos2, pos3, out
+):
+    nc = tc.nc
+    with ExitStack() as ctx:
+        held = ctx.enter_context(tc.tile_pool(name="held", bufs=1))
+        psum = ctx.enter_context(tc.psum_pool(name="psum", bufs=8))
+
+        offs_t = held.tile([P, S // 16], U16, name="offs_t")
+        pos_t = [held.tile([P, T // 16], U16, name=f"pos_t{r}") for r in range(TOP)]
+
+        planes = held.tile([P, 2 * T], U8, name="planes", align_bytes=64)
+        codes = [
+            held.tile([P, 2 * T if a < PASSES - 1 else T], U32, name=f"codes{a}", align_bytes=64) for a in range(PASSES)
+        ]
+        low = [held.tile([P, S], U8, name=f"low{i}", align_bytes=64) for i in range(2)]
+        ws8 = held.tile([P, E, N], U8, name="ws8", align_bytes=64)
+        ws4 = held.tile([P, 2 * E, N], U8, name="ws4", align_bytes=64)
+        warm = held.tile([P, 1], F32, name="warm")
+        nc.vector.memset(warm[:], 0.0)
+        nc.gpsimd.memset(planes[:].bitcast(I32), 0)
+        nc.gpsimd.memset(ws8[:].rearrange("p e n -> p (e n)").bitcast(I32), 0)
+        nc.gpsimd.memset(ws4[:].rearrange("p e n -> p (e n)").bitcast(I32), 0)
+        for a in range(PASSES - 1):
+            nc.vector.memset(codes[a][:, T : 2 * T].bitcast(I32), 0)
+        for i in range(2):
+            nc.vector.memset(low[i][96:128, :].bitcast(I32), 0)
+        warm_out = held.tile([P, 1], F32, name="warm_out")
+        nc.scalar.activation(out=warm_out[:], in_=warm[:], func=SILU)
+
+        chunks = [(a, t0, n) for a in range(PASSES) for n in ((256,) if a == 0 else (512,)) for t0 in range(0, T, n)]
+        raw = {}
+        for a, t0, n in chunks:
+            r = held.tile([P, 4, n], F32, name=f"raw{a}_{t0}")
+            nc.sync.dma_start(
+                out=r[:], in_=xT[512 * a : 512 * a + 512, t0 : t0 + n].rearrange("(p j) t -> p j t", j=4)
+            )
+            raw[a, t0] = r
+            if a == 0 and t0 == 768:
+                nc.sync.dma_start(offs_t[:], offs)
+        w8 = held.tile([P, E, 4 * N], U8, name="w8", align_bytes=64)
+        nc.sync.dma_start(out=w8[:].bitcast(I32), in_=w8_words.rearrange("e a p n r -> p (e a) (n r)").bitcast(I32))
+        w4 = held.tile([P, 2 * E, 2 * N], U8, name="w4", align_bytes=64)
+        nc.sync.dma_start(out=w4[:].bitcast(I32), in_=w4_words.rearrange("e a p m -> p (e a) m").bitcast(I32))
+        for q in range(4):
+            nc.sync.dma_start(
+                out=ws8[32 * q : 32 * q + 4, :, :].bitcast(I32),
+                in_=w8_scales[:, 0, 4 * q : 4 * q + 4, :].rearrange("e q n -> q e n").bitcast(I32),
+            )
+            nc.sync.dma_start(
+                out=ws4[32 * q : 32 * q + 4, :, :].bitcast(I32),
+                in_=w4_scales[:, :, 4 * q : 4 * q + 4, :].rearrange("e a q n -> q (e a) n").bitcast(I32),
+            )
+        bias = held.tile([P, E], F32, name="bias")
+        nc.sync.dma_start(out=bias[:], in_=b)
+        for r, pos in enumerate((pos1, pos2, pos3)):
+            nc.sync.dma_start(pos_t[r][:], pos)
+        gates = [held.tile([P, T], F32, name=f"gate{r}") for r in range(TOP)]
+        for r in range(TOP):
+            nc.sync.dma_start(out=gates[r][:], in_=gate[r])
+
+        slot_codes = [held.tile([P, S], U32, name=f"slot_codes{a}", align_bytes=64) for a in range(PASSES)]
+        slot_planes = held.tile([P, S], U8, name="slot_planes", align_bytes=64)
+
+        def gather_codes(a):
+            s0 = 0
+            for cut in (768, 768, 768, 512, 128, 128) if a == PASSES - 1 else (1536, 1536):
+                nc.vector.tensor_copy(
+                    out=slot_codes[a][:, s0 : s0 + cut],
+                    in_=codes[a][:].indirect(offs_t[:, s0 // 16 : (s0 + cut) // 16]),
+                )
+                s0 += cut
+
+        for a in range(PASSES):
+            for a2, t0, n in chunks:
+                if a2 != a:
+                    continue
+                grouped = held.tile([P, n, 4], BF16, name=f"grouped{a}_{t0}", align_bytes=64)
+                src = raw[a, t0][:].rearrange("p j t -> p t j")
+                if a == 0 and t0 == 768:
+                    nc.scalar.activation(out=grouped[:, 128:256, :], in_=src[:, 128:256, :], func=COPY)
+                    nc.vector.tensor_copy(out=grouped[:, 0:128, :], in_=src[:, 0:128, :])
+                    for u in (0, 128):
+                        nc.vector.quantize_mx(
+                            out=codes[a][:, t0 + u : t0 + u + 128].bitcast(FP8X4),
+                            scales=planes[4 * a : P, t0 + u : t0 + u + 128],
+                            in_=grouped[:, u : u + 128, :].rearrange("p t j -> p (t j)"),
+                        )
+                    continue
+                if a == 0:
+                    nc.vector.tensor_copy(out=grouped[:], in_=src)
+                else:
+                    nc.scalar.activation(out=grouped[:], in_=src, func=COPY)
+                nc.vector.quantize_mx(
+                    out=codes[a][:, t0 : t0 + n].bitcast(FP8X4),
+                    scales=planes[4 * a : P, t0 : t0 + n],
+                    in_=grouped[:].rearrange("p t j -> p (t j)"),
+                )
+            if a < PASSES - 1:
+                gather_codes(a)
+        for s0 in range(0, S, CUT):
+            nc.vector.tensor_copy(
+                out=slot_planes[:, s0 : s0 + CUT], in_=planes[:].indirect(offs_t[:, s0 // 16 : (s0 + CUT) // 16])
+            )
+            for i in range(2):
+                shift = 4 * (i + 1)
+                nc.sync.dma_start(
+                    out=low[i][0 : P - shift, s0 : s0 + CUT].bitcast(I32),
+                    in_=slot_planes[shift:P, s0 : s0 + CUT].bitcast(I32),
+                )
+        gather_codes(PASSES - 1)
+
+        y = held.tile([P, S], F32, name="y")
+        for e in range(E):
+            acc = psum.tile([P, C], F32, name="acc")
+            for h in range(C // 128):
+                cols = slice(C * e + 128 * h, C * e + 128 * h + 128)
+                for a in range(PASSES):
+                    if a == 0:
+                        lhsT, lhsT_scale = w8[:, e, :].bitcast(FP8X4), ws8[:, e, :]
+                        rhs_scale = slot_planes[:, cols]
+                    else:
+                        m = 2 * e + a - 1
+                        lhsT, lhsT_scale = w4[:, m, :].bitcast(FP4X4), ws4[:, m, :]
+                        rhs_scale = low[a - 1][:, cols]
+                    nc.tensor.matmul_mx(
+                        out=acc[:, 128 * h : 128 * h + 128],
+                        lhsT=lhsT,
+                        lhsT_scale=lhsT_scale,
+                        rhs=slot_codes[a][:, cols].bitcast(FP8X4),
+                        rhs_scale=rhs_scale,
+                        start=(a == 0),
+                        stop=(a == PASSES - 1),
+                    )
+            for h0, h1 in ((0, C),) if e < E - 1 else ((0, 128), (128, C)):
+                nc.scalar.activation(
+                    out=y[:, C * e + h0 : C * e + h1], in_=acc[:, h0:h1], func=SILU, bias=bias[:, e : e + 1]
+                )
+
+        CUT_T = 640
+        parts = {}
+
+        def fetch(t0, t1, r):
+            g = held.tile([P, t1 - t0], F32, name=f"part{r}_{t0}")
+            nc.vector.tensor_tensor(g[:], y[:].indirect(pos_t[r][:, t0 // 16 : t1 // 16]), gates[r][:, t0:t1], MULT)
+            parts[t0, r] = g
+
+        def add01(t0, t1):
+            s = held.tile([P, t1 - t0], F32, name=f"sum_{t0}")
+            nc.vector.tensor_add(s[:], parts[t0, 0][:], parts[t0, 1][:])
+            parts[t0, 3] = s
+
+        def add2(t0, t1):
+            o = held.tile([P, t1 - t0], F32, name=f"out_{t0}")
+            nc.vector.tensor_add(o[:], parts[t0, 3][:], parts[t0, 2][:])
+            nc.sync.dma_start(out=out[:, t0:t1], in_=o[:])
+
+        for r in range(TOP):
+            fetch(0, CUT_T, r)
+        add01(0, CUT_T)
+        fetch(CUT_T, T, 0)
+        add2(0, CUT_T)
+        fetch(CUT_T, T, 1)
+        fetch(CUT_T, T, 2)
+        add01(CUT_T, T)
+        add2(CUT_T, T)

@@ -22,6 +22,7 @@ SILU = mybir.ActivationFunctionType.Silu
 MULT = mybir.AluOpType.mult
 
 CUT = 1536
+PLANE = (4, 0, 8)
 
 
 def tile_moe_tk_lin_silu_kernel(
@@ -39,7 +40,7 @@ def tile_moe_tk_lin_silu_kernel(
         codes = [
             held.tile([P, 2 * T if a < PASSES - 1 else T], U32, name=f"codes{a}", align_bytes=64) for a in range(PASSES)
         ]
-        low = [held.tile([P, S], U8, name=f"low{i}", align_bytes=64) for i in range(2)]
+        low = held.tile([P, S], U8, name="low", align_bytes=64)
         ws8 = held.tile([P, E, N], U8, name="ws8", align_bytes=64)
         ws4 = held.tile([P, 2 * E, N], U8, name="ws4", align_bytes=64)
         warm = held.tile([P, 1], F32, name="warm")
@@ -49,12 +50,11 @@ def tile_moe_tk_lin_silu_kernel(
         nc.gpsimd.memset(ws4[:].rearrange("p e n -> p (e n)").bitcast(I32), 0)
         for a in range(PASSES - 1):
             nc.vector.memset(codes[a][:, T : 2 * T].bitcast(I32), 0)
-        for i in range(2):
-            nc.vector.memset(low[i][96:128, :].bitcast(I32), 0)
+        nc.gpsimd.memset(low[:].bitcast(I32), 0)
         warm_out = held.tile([P, 1], F32, name="warm_out")
         nc.scalar.activation(out=warm_out[:], in_=warm[:], func=SILU)
 
-        chunks = [(a, t0, n) for a in range(PASSES) for n in ((256,) if a == 0 else (512,)) for t0 in range(0, T, n)]
+        chunks = [(0, 0, 512), (0, 512, 256), (0, 768, 256)] + [(a, t0, 512) for a in (1, 2) for t0 in (0, 512)]
         raw = {}
         for a, t0, n in chunks:
             r = held.tile([P, 4, n], F32, name=f"raw{a}_{t0}")
@@ -88,53 +88,52 @@ def tile_moe_tk_lin_silu_kernel(
         slot_codes = [held.tile([P, S], U32, name=f"slot_codes{a}", align_bytes=64) for a in range(PASSES)]
         slot_planes = held.tile([P, S], U8, name="slot_planes", align_bytes=64)
 
-        def gather_codes(a):
-            s0 = 0
-            for cut in (768, 768, 768, 512, 128, 128) if a == PASSES - 1 else (1536, 1536):
-                nc.vector.tensor_copy(
-                    out=slot_codes[a][:, s0 : s0 + cut],
-                    in_=codes[a][:].indirect(offs_t[:, s0 // 16 : (s0 + cut) // 16]),
-                )
-                s0 += cut
+        def gather_codes(a, s0, s1):
+            nc.vector.tensor_copy(out=slot_codes[a][:, s0:s1], in_=codes[a][:].indirect(offs_t[:, s0 // 16 : s1 // 16]))
 
-        for a in range(PASSES):
-            for a2, t0, n in chunks:
-                if a2 != a:
-                    continue
-                grouped = held.tile([P, n, 4], BF16, name=f"grouped{a}_{t0}", align_bytes=64)
-                src = raw[a, t0][:].rearrange("p j t -> p t j")
-                if a == 0 and t0 == 768:
-                    nc.scalar.activation(out=grouped[:, 128:256, :], in_=src[:, 128:256, :], func=COPY)
-                    nc.vector.tensor_copy(out=grouped[:, 0:128, :], in_=src[:, 0:128, :])
-                    for u in (0, 128):
-                        nc.vector.quantize_mx(
-                            out=codes[a][:, t0 + u : t0 + u + 128].bitcast(FP8X4),
-                            scales=planes[4 * a : P, t0 + u : t0 + u + 128],
-                            in_=grouped[:, u : u + 128, :].rearrange("p t j -> p (t j)"),
-                        )
-                    continue
-                if a == 0:
-                    nc.vector.tensor_copy(out=grouped[:], in_=src)
-                else:
-                    nc.scalar.activation(out=grouped[:], in_=src, func=COPY)
-                nc.vector.quantize_mx(
-                    out=codes[a][:, t0 : t0 + n].bitcast(FP8X4),
-                    scales=planes[4 * a : P, t0 : t0 + n],
-                    in_=grouped[:].rearrange("p t j -> p (t j)"),
-                )
-            if a < PASSES - 1:
-                gather_codes(a)
+        def round_and_quantise(a, t0, n, on_scalar):
+            grouped = held.tile([P, n, 4], BF16, name=f"grouped{a}_{t0}", align_bytes=64)
+            src = raw[a, t0][:].rearrange("p j t -> p t j")
+            v = n - on_scalar
+            if on_scalar:
+                nc.scalar.activation(out=grouped[:, v:n, :], in_=src[:, v:n, :], func=COPY)
+            if v:
+                nc.vector.tensor_copy(out=grouped[:, 0:v, :], in_=src[:, 0:v, :])
+            for u0, u1 in ((0, v), (v, n)):
+                if u0 < u1:
+                    nc.vector.quantize_mx(
+                        out=codes[a][:, t0 + u0 : t0 + u1].bitcast(FP8X4),
+                        scales=planes[PLANE[a] : P, t0 + u0 : t0 + u1],
+                        in_=grouped[:, u0:u1, :].rearrange("p t j -> p (t j)"),
+                    )
+
+        round_and_quantise(0, 0, 512, 256)
+        round_and_quantise(0, 512, 256, 0)
+        round_and_quantise(0, 768, 256, 128)
+        gather_codes(0, 0, 1536)
+        gather_codes(0, 1536, 3072)
+        round_and_quantise(1, 0, 512, 512)
+        round_and_quantise(1, 512, 512, 512)
+        gather_codes(1, 0, 1536)
+        gather_codes(1, 1536, 2304)
+        round_and_quantise(2, 0, 512, 512)
+        round_and_quantise(2, 512, 512, 512)
         for s0 in range(0, S, CUT):
             nc.vector.tensor_copy(
                 out=slot_planes[:, s0 : s0 + CUT], in_=planes[:].indirect(offs_t[:, s0 // 16 : (s0 + CUT) // 16])
             )
-            for i in range(2):
-                shift = 4 * (i + 1)
+            for q in range(4):
                 nc.sync.dma_start(
-                    out=low[i][0 : P - shift, s0 : s0 + CUT].bitcast(I32),
-                    in_=slot_planes[shift:P, s0 : s0 + CUT].bitcast(I32),
+                    out=low[32 * q : 32 * q + 4, s0 : s0 + CUT].bitcast(I32),
+                    in_=slot_planes[32 * q + 8 : 32 * q + 12, s0 : s0 + CUT].bitcast(I32),
                 )
-        gather_codes(PASSES - 1)
+        gather_codes(2, 0, 768)
+        gather_codes(2, 768, 1536)
+        gather_codes(2, 1536, 2304)
+        gather_codes(1, 2304, 3072)
+        gather_codes(2, 2304, 2816)
+        gather_codes(2, 2816, 2944)
+        gather_codes(2, 2944, 3072)
 
         y = held.tile([P, S], F32, name="y")
         for e in range(E):
@@ -144,11 +143,10 @@ def tile_moe_tk_lin_silu_kernel(
                 for a in range(PASSES):
                     if a == 0:
                         lhsT, lhsT_scale = w8[:, e, :].bitcast(FP8X4), ws8[:, e, :]
-                        rhs_scale = slot_planes[:, cols]
                     else:
                         m = 2 * e + a - 1
                         lhsT, lhsT_scale = w4[:, m, :].bitcast(FP4X4), ws4[:, m, :]
-                        rhs_scale = low[a - 1][:, cols]
+                    rhs_scale = low[:, cols] if a == 2 else slot_planes[PLANE[a] : P, cols]
                     nc.tensor.matmul_mx(
                         out=acc[:, 128 * h : 128 * h + 128],
                         lhsT=lhsT,
@@ -163,7 +161,7 @@ def tile_moe_tk_lin_silu_kernel(
                     out=y[:, C * e + h0 : C * e + h1], in_=acc[:, h0:h1], func=SILU, bias=bias[:, e : e + 1]
                 )
 
-        CUT_T = 640
+        CUT_T = 768
         parts = {}
 
         def fetch(t0, t1, r):

@@ -64,10 +64,6 @@ def tile_moe_tk_lin_silu_kernel(
             raw[a, t0] = r
             if a == 0 and t0 == 768:
                 nc.sync.dma_start(offs_t[:], offs)
-        w8 = held.tile([P, E, 4 * N], U8, name="w8", align_bytes=64)
-        nc.sync.dma_start(out=w8[:].bitcast(I32), in_=w8_words.rearrange("e a p n r -> p (e a) (n r)").bitcast(I32))
-        w4 = held.tile([P, 2 * E, 2 * N], U8, name="w4", align_bytes=64)
-        nc.sync.dma_start(out=w4[:].bitcast(I32), in_=w4_words.rearrange("e a p m -> p (e a) m").bitcast(I32))
         for q in range(4):
             nc.sync.dma_start(
                 out=ws8[32 * q : 32 * q + 4, :, :].bitcast(I32),
@@ -77,13 +73,14 @@ def tile_moe_tk_lin_silu_kernel(
                 out=ws4[32 * q : 32 * q + 4, :, :].bitcast(I32),
                 in_=w4_scales[:, :, 4 * q : 4 * q + 4, :].rearrange("e a q n -> q (e a) n").bitcast(I32),
             )
+        w8 = held.tile([P, E, 4 * N], U8, name="w8", align_bytes=64)
+        nc.sync.dma_start(out=w8[:].bitcast(I32), in_=w8_words.rearrange("e a p n r -> p (e a) (n r)").bitcast(I32))
+        w4 = held.tile([P, 2 * E, 2 * N], U8, name="w4", align_bytes=64)
+        nc.sync.dma_start(out=w4[:].bitcast(I32), in_=w4_words.rearrange("e a p m -> p (e a) m").bitcast(I32))
         bias = held.tile([P, E], F32, name="bias")
         nc.sync.dma_start(out=bias[:], in_=b)
         for r, pos in enumerate((pos1, pos2, pos3)):
             nc.sync.dma_start(pos_t[r][:], pos)
-        gates = [held.tile([P, T], F32, name=f"gate{r}") for r in range(TOP)]
-        for r in range(TOP):
-            nc.sync.dma_start(out=gates[r][:], in_=gate[r])
 
         slot_codes = [held.tile([P, S], U32, name=f"slot_codes{a}", align_bytes=64) for a in range(PASSES)]
         slot_planes = held.tile([P, S], U8, name="slot_planes", align_bytes=64)
@@ -92,13 +89,19 @@ def tile_moe_tk_lin_silu_kernel(
             nc.vector.tensor_copy(out=slot_codes[a][:, s0:s1], in_=codes[a][:].indirect(offs_t[:, s0 // 16 : s1 // 16]))
 
         def round_and_quantise(a, t0, n, on_scalar):
-            grouped = held.tile([P, n, 4], BF16, name=f"grouped{a}_{t0}", align_bytes=64)
-            src = raw[a, t0][:].rearrange("p j t -> p t j")
+            grouped = held.tile([P, n, 4], BF16, name=f"grouped{a}_{t0}", tag="late" if (a, t0) == (2, 512) else f"grouped{a}_{t0}", align_bytes=64)
             v = n - on_scalar
             if on_scalar:
-                nc.scalar.activation(out=grouped[:, v:n, :], in_=src[:, v:n, :], func=COPY)
+                nc.scalar.activation(
+                    out=grouped[:, v:n, :].rearrange("p (c i) j -> p c j i", i=4),
+                    in_=raw[a, t0][:, :, v:n].rearrange("p j (c i) -> p c j i", i=4),
+                    func=COPY,
+                )
             if v:
-                nc.vector.tensor_copy(out=grouped[:, 0:v, :], in_=src[:, 0:v, :])
+                nc.vector.tensor_copy(
+                    out=grouped[:, 0:v, :].rearrange("p (c i) j -> p c j i", i=4),
+                    in_=raw[a, t0][:, :, 0:v].rearrange("p j (c i) -> p c j i", i=4),
+                )
             for u0, u1 in ((0, v), (v, n)):
                 if u0 < u1:
                     nc.vector.quantize_mx(
@@ -115,58 +118,59 @@ def tile_moe_tk_lin_silu_kernel(
         round_and_quantise(1, 0, 512, 512)
         round_and_quantise(1, 512, 512, 512)
         gather_codes(1, 0, 1536)
-        gather_codes(1, 1536, 2304)
+        gather_codes(1, 1536, 3072)
         round_and_quantise(2, 0, 512, 512)
         round_and_quantise(2, 512, 512, 512)
-        for s0 in range(0, S, CUT):
-            nc.vector.tensor_copy(
-                out=slot_planes[:, s0 : s0 + CUT], in_=planes[:].indirect(offs_t[:, s0 // 16 : (s0 + CUT) // 16])
-            )
+        gates = held.tile([P, TOP, T], F32, name="gates", tag="late", align_bytes=64)
+        nc.scalar.dma_start(out=gates[:], in_=gate.rearrange("r p t -> p r t"))
+
+        def gather_bytes(s0, s1):
+            nc.vector.tensor_copy(out=slot_planes[:, s0:s1], in_=planes[:].indirect(offs_t[:, s0 // 16 : s1 // 16]))
             for q in range(4):
                 nc.sync.dma_start(
-                    out=low[32 * q : 32 * q + 4, s0 : s0 + CUT].bitcast(I32),
-                    in_=slot_planes[32 * q + 8 : 32 * q + 12, s0 : s0 + CUT].bitcast(I32),
+                    out=low[32 * q : 32 * q + 4, s0:s1].bitcast(I32),
+                    in_=slot_planes[32 * q + 8 : 32 * q + 12, s0:s1].bitcast(I32),
                 )
+
+        gather_bytes(0, 768)
         gather_codes(2, 0, 768)
+        gather_bytes(768, 1536)
         gather_codes(2, 768, 1536)
+        gather_bytes(1536, 2304)
+        gather_bytes(2304, 3072)
         gather_codes(2, 1536, 2304)
-        gather_codes(1, 2304, 3072)
         gather_codes(2, 2304, 2816)
         gather_codes(2, 2816, 2944)
         gather_codes(2, 2944, 3072)
 
         y = held.tile([P, S], F32, name="y")
-        for e in range(E):
-            acc = psum.tile([P, C], F32, name="acc")
-            for h in range(C // 128):
-                cols = slice(C * e + 128 * h, C * e + 128 * h + 128)
-                for a in range(PASSES):
-                    if a == 0:
-                        lhsT, lhsT_scale = w8[:, e, :].bitcast(FP8X4), ws8[:, e, :]
-                    else:
-                        m = 2 * e + a - 1
-                        lhsT, lhsT_scale = w4[:, m, :].bitcast(FP4X4), ws4[:, m, :]
-                    rhs_scale = low[:, cols] if a == 2 else slot_planes[PLANE[a] : P, cols]
-                    nc.tensor.matmul_mx(
-                        out=acc[:, 128 * h : 128 * h + 128],
-                        lhsT=lhsT,
-                        lhsT_scale=lhsT_scale,
-                        rhs=slot_codes[a][:, cols].bitcast(FP8X4),
-                        rhs_scale=rhs_scale,
-                        start=(a == 0),
-                        stop=(a == PASSES - 1),
-                    )
-            for h0, h1 in ((0, C),) if e < E - 1 else ((0, 128), (128, C)):
-                nc.scalar.activation(
-                    out=y[:, C * e + h0 : C * e + h1], in_=acc[:, h0:h1], func=SILU, bias=bias[:, e : e + 1]
+        for s0 in range(0, S, 128):
+            e = s0 // C
+            cols = slice(s0, s0 + 128)
+            acc = psum.tile([P, 128], F32, name="acc")
+            for a in range(PASSES):
+                if a == 0:
+                    lhsT, lhsT_scale = w8[:, e, :].bitcast(FP8X4), ws8[:, e, :]
+                else:
+                    m = 2 * e + a - 1
+                    lhsT, lhsT_scale = w4[:, m, :].bitcast(FP4X4), ws4[:, m, :]
+                nc.tensor.matmul_mx(
+                    out=acc[:],
+                    lhsT=lhsT,
+                    lhsT_scale=lhsT_scale,
+                    rhs=slot_codes[a][:, cols].bitcast(FP8X4),
+                    rhs_scale=low[:, cols] if a == 2 else slot_planes[PLANE[a] : P, cols],
+                    start=(a == 0),
+                    stop=(a == PASSES - 1),
                 )
+            nc.scalar.activation(out=y[:, cols], in_=acc[:], func=SILU, bias=bias[:, e : e + 1])
 
         CUT_T = 768
         parts = {}
 
         def fetch(t0, t1, r):
             g = held.tile([P, t1 - t0], F32, name=f"part{r}_{t0}")
-            nc.vector.tensor_tensor(g[:], y[:].indirect(pos_t[r][:, t0 // 16 : t1 // 16]), gates[r][:, t0:t1], MULT)
+            nc.vector.tensor_tensor(g[:], y[:].indirect(pos_t[r][:, t0 // 16 : t1 // 16]), gates[:, r, t0:t1], MULT)
             parts[t0, r] = g
 
         def add01(t0, t1):

@@ -114,11 +114,12 @@ def tile_moe_tk_lin_silu_kernel(
         round_and_quantise(0, 512, 256, 0)
         round_and_quantise(0, 768, 256, 128)
         gather_codes(0, 0, 1536)
-        gather_codes(0, 1536, 3072)
+        gather_codes(0, 1536, 2688)
         round_and_quantise(1, 0, 512, 512)
         round_and_quantise(1, 512, 512, 512)
+        gather_codes(0, 2688, 3072)
         gather_codes(1, 0, 1536)
-        gather_codes(1, 1536, 3072)
+        gather_codes(1, 1536, 2304)
         round_and_quantise(2, 0, 512, 512)
         round_and_quantise(2, 512, 512, 512)
         gates = held.tile([P, TOP, T], F32, name="gates", tag="late", align_bytes=64)
@@ -139,6 +140,7 @@ def tile_moe_tk_lin_silu_kernel(
         gather_bytes(1536, 2304)
         gather_bytes(2304, 3072)
         gather_codes(2, 1536, 2304)
+        gather_codes(1, 2304, 3072)
         gather_codes(2, 2304, 2816)
         gather_codes(2, 2816, 2944)
         gather_codes(2, 2944, 3072)
@@ -165,30 +167,25 @@ def tile_moe_tk_lin_silu_kernel(
                 )
             nc.scalar.activation(out=y[:, cols], in_=acc[:], func=SILU, bias=bias[:, e : e + 1])
 
-        CUT_T = 768
-        parts = {}
+        parts = [held.tile([P, T], F32, name=f"part{r}") for r in range(TOP)]
+        total = held.tile([P, T], F32, name="total")
+        result = held.tile([P, T], F32, name="result")
 
-        def fetch(t0, t1, r):
-            g = held.tile([P, t1 - t0], F32, name=f"part{r}_{t0}")
-            nc.vector.tensor_tensor(g[:], y[:].indirect(pos_t[r][:, t0 // 16 : t1 // 16]), gates[:, r, t0:t1], MULT)
-            parts[t0, r] = g
+        def fetch(r, t0, t1):
+            nc.vector.tensor_tensor(
+                parts[r][:, t0:t1], y[:].indirect(pos_t[r][:, t0 // 16 : t1 // 16]), gates[:, r, t0:t1], MULT
+            )
 
-        def add01(t0, t1):
-            s = held.tile([P, t1 - t0], F32, name=f"sum_{t0}")
-            nc.vector.tensor_add(s[:], parts[t0, 0][:], parts[t0, 1][:])
-            parts[t0, 3] = s
+        def finish(t0, t1):
+            nc.vector.tensor_add(result[:, t0:t1], total[:, t0:t1], parts[2][:, t0:t1])
+            nc.sync.dma_start(out=out[:, t0:t1], in_=result[:, t0:t1])
 
-        def add2(t0, t1):
-            o = held.tile([P, t1 - t0], F32, name=f"out_{t0}")
-            nc.vector.tensor_add(o[:], parts[t0, 3][:], parts[t0, 2][:])
-            nc.sync.dma_start(out=out[:, t0:t1], in_=o[:])
-
-        for r in range(TOP):
-            fetch(0, CUT_T, r)
-        add01(0, CUT_T)
-        fetch(CUT_T, T, 0)
-        add2(0, CUT_T)
-        fetch(CUT_T, T, 1)
-        fetch(CUT_T, T, 2)
-        add01(CUT_T, T)
-        add2(CUT_T, T)
+        fetch(0, 0, T)
+        fetch(1, 0, T)
+        fetch(2, 0, 512)
+        nc.vector.tensor_add(total[:], parts[0][:], parts[1][:])
+        fetch(2, 512, 768)
+        finish(0, 512)
+        fetch(2, 768, T)
+        finish(512, 768)
+        finish(768, T)

@@ -48,13 +48,11 @@ def tile_moe_tk_lin_silu_kernel(
         nc.gpsimd.memset(planes[:].bitcast(I32), 0)
         nc.gpsimd.memset(ws8[:].rearrange("p e n -> p (e n)").bitcast(I32), 0)
         nc.gpsimd.memset(ws4[:].rearrange("p e n -> p (e n)").bitcast(I32), 0)
-        for a in range(PASSES - 1):
-            nc.vector.memset(codes[a][:, T : 2 * T].bitcast(I32), 0)
         nc.gpsimd.memset(low[:].bitcast(I32), 0)
         warm_out = held.tile([P, 1], F32, name="warm_out")
         nc.scalar.activation(out=warm_out[:], in_=warm[:], func=SILU)
 
-        chunks = [(0, 0, 512), (0, 512, 256), (0, 768, 256)] + [(a, t0, 512) for a in (1, 2) for t0 in (0, 512)]
+        chunks = [(0, t0, 256) for t0 in range(0, T, 256)] + [(a, t0, 512) for a in (1, 2) for t0 in (0, 512)]
         raw = {}
         for a, t0, n in chunks:
             r = held.tile([P, 4, n], F32, name=f"raw{a}_{t0}")
@@ -82,14 +80,17 @@ def tile_moe_tk_lin_silu_kernel(
         for r, pos in enumerate((pos1, pos2, pos3)):
             nc.sync.dma_start(pos_t[r][:], pos)
 
-        slot_codes = [held.tile([P, S], U32, name=f"slot_codes{a}", align_bytes=64) for a in range(PASSES)]
+        HELD_BACK = 2304
+        slot_codes = [
+            held.tile([P, HELD_BACK if a == 1 else S], U32, name=f"slot_codes{a}", align_bytes=64) for a in range(PASSES)
+        ]
         slot_planes = held.tile([P, S], U8, name="slot_planes", align_bytes=64)
 
         def gather_codes(a, s0, s1):
             nc.vector.tensor_copy(out=slot_codes[a][:, s0:s1], in_=codes[a][:].indirect(offs_t[:, s0 // 16 : s1 // 16]))
 
         def round_and_quantise(a, t0, n, on_scalar):
-            grouped = held.tile([P, n, 4], BF16, name=f"grouped{a}_{t0}", tag="late" if (a, t0) == (2, 512) else f"grouped{a}_{t0}", align_bytes=64)
+            grouped = held.tile([P, n, 4], BF16, name=f"grouped{a}_{t0}", tag={(2, 0): "late", (2, 512): "later"}.get((a, t0), f"grouped{a}_{t0}"), align_bytes=64)
             v = n - on_scalar
             if on_scalar:
                 nc.scalar.activation(
@@ -110,7 +111,8 @@ def tile_moe_tk_lin_silu_kernel(
                         in_=grouped[:, u0:u1, :].rearrange("p t j -> p (t j)"),
                     )
 
-        round_and_quantise(0, 0, 512, 256)
+        round_and_quantise(0, 0, 256, 0)
+        round_and_quantise(0, 256, 256, 256)
         round_and_quantise(0, 512, 256, 0)
         round_and_quantise(0, 768, 256, 128)
         gather_codes(0, 0, 1536)
@@ -135,12 +137,12 @@ def tile_moe_tk_lin_silu_kernel(
 
         gather_bytes(0, 768)
         gather_codes(2, 0, 768)
-        gather_bytes(768, 1536)
+        gather_bytes(768, 2304)
         gather_codes(2, 768, 1536)
-        gather_bytes(1536, 2304)
         gather_bytes(2304, 3072)
         gather_codes(2, 1536, 2304)
-        gather_codes(1, 2304, 3072)
+        late_codes = held.tile([P, S - HELD_BACK], U32, name="late_codes", tag="later", align_bytes=64)
+        nc.vector.tensor_copy(out=late_codes[:], in_=codes[1][:].indirect(offs_t[:, HELD_BACK // 16 : S // 16]))
         gather_codes(2, 2304, 2816)
         gather_codes(2, 2816, 2944)
         gather_codes(2, 2944, 3072)
@@ -160,7 +162,11 @@ def tile_moe_tk_lin_silu_kernel(
                     out=acc[:],
                     lhsT=lhsT,
                     lhsT_scale=lhsT_scale,
-                    rhs=slot_codes[a][:, cols].bitcast(FP8X4),
+                    rhs=(
+                        late_codes[:, s0 - HELD_BACK : s0 - HELD_BACK + 128]
+                        if a == 1 and s0 >= HELD_BACK
+                        else slot_codes[a][:, cols]
+                    ).bitcast(FP8X4),
                     rhs_scale=low[:, cols] if a == 2 else slot_planes[PLANE[a] : P, cols],
                     start=(a == 0),
                     stop=(a == PASSES - 1),

from contextlib import ExitStack

import concourse.mybir as mybir

K, T, E, C, N = 1536, 1024, 12, 256, 128
TOP = 3
S = E * C
PASSES = 3
P = 128
FLOPS = 2 * S * K * N

F32 = mybir.dt.float32
BF16 = mybir.dt.bfloat16
I32 = mybir.dt.int32
U32 = mybir.dt.uint32
U16 = mybir.dt.uint16
U8 = mybir.dt.uint8
FP8X4 = mybir.dt.float8_e4m3fn_x4
FP4X4 = mybir.dt.float4_e2m1fn_x4
COPY = mybir.ActivationFunctionType.Copy
SILU = mybir.ActivationFunctionType.Silu
MULT = mybir.AluOpType.mult

CUT = 1536
PLANE = (4, 0, 8)


def tile_moe_tk_lin_silu_kernel(
    tc, xT, w8_words, w8_scales, w4_words, w4_scales, b, gate, offs, pos1, pos2, pos3, out
):
    nc = tc.nc
    with ExitStack() as ctx:
        held = ctx.enter_context(tc.tile_pool(name="held", bufs=1))
        psum = ctx.enter_context(tc.psum_pool(name="psum", bufs=8))

        offs_t = held.tile([P, S // 16], U16, name="offs_t")
        pos_t = [held.tile([P, T // 16], U16, name=f"pos_t{r}") for r in range(TOP)]

        planes = held.tile([P, 2 * T], U8, name="planes", align_bytes=64)
        codes = [
            held.tile([P, 2 * T if a < PASSES - 1 else T], U32, name=f"codes{a}", align_bytes=64) for a in range(PASSES)
        ]
        low = held.tile([P, S], U8, name="low", align_bytes=64)
        ws8 = held.tile([P, E, N], U8, name="ws8", align_bytes=64)
        ws4 = held.tile([P, 2 * E, N], U8, name="ws4", align_bytes=64)
        warm = held.tile([P, 1], F32, name="warm")
        nc.vector.memset(warm[:], 0.0)
        nc.gpsimd.memset(planes[:].bitcast(I32), 0)
        nc.gpsimd.memset(ws8[:].rearrange("p e n -> p (e n)").bitcast(I32), 0)
        nc.gpsimd.memset(ws4[:].rearrange("p e n -> p (e n)").bitcast(I32), 0)
        nc.gpsimd.memset(low[:].bitcast(I32), 0)
        warm_out = held.tile([P, 1], F32, name="warm_out")
        nc.scalar.activation(out=warm_out[:], in_=warm[:], func=SILU)

        chunks = [(0, t0, 256) for t0 in range(0, T, 256)] + [(a, t0, 512) for a in (1, 2) for t0 in (0, 512)]
        raw = {}
        for a, t0, n in chunks:
            r = held.tile([P, 4, n], F32, name=f"raw{a}_{t0}")
            nc.sync.dma_start(
                out=r[:], in_=xT[512 * a : 512 * a + 512, t0 : t0 + n].rearrange("(p j) t -> p j t", j=4)
            )
            raw[a, t0] = r
            if a == 0 and t0 == 768:
                nc.sync.dma_start(offs_t[:], offs)
        for q in range(4):
            nc.sync.dma_start(
                out=ws8[32 * q : 32 * q + 4, :, :].bitcast(I32),
                in_=w8_scales[:, 0, 4 * q : 4 * q + 4, :].rearrange("e q n -> q e n").bitcast(I32),
            )
            nc.sync.dma_start(
                out=ws4[32 * q : 32 * q + 4, :, :].bitcast(I32),
                in_=w4_scales[:, :, 4 * q : 4 * q + 4, :].rearrange("e a q n -> q (e a) n").bitcast(I32),
            )
        w8 = held.tile([P, E, 4 * N], U8, name="w8", align_bytes=64)
        nc.sync.dma_start(out=w8[:].bitcast(I32), in_=w8_words.rearrange("e a p n r -> p (e a) (n r)").bitcast(I32))
        w4 = held.tile([P, 2 * E, 2 * N], U8, name="w4", align_bytes=64)
        nc.sync.dma_start(out=w4[:].bitcast(I32), in_=w4_words.rearrange("e a p m -> p (e a) m").bitcast(I32))
        bias = held.tile([P, E], F32, name="bias")
        nc.sync.dma_start(out=bias[:], in_=b)
        for r, pos in enumerate((pos1, pos2, pos3)):
            nc.sync.dma_start(pos_t[r][:], pos)

        HELD_BACK = 2304
        slot_codes = [
            held.tile([P, HELD_BACK if a == 1 else S], U32, name=f"slot_codes{a}", align_bytes=64) for a in range(PASSES)
        ]
        slot_planes = held.tile([P, S], U8, name="slot_planes", align_bytes=64)

        def gather_codes(a, s0, s1):
            nc.vector.tensor_copy(out=slot_codes[a][:, s0:s1], in_=codes[a][:].indirect(offs_t[:, s0 // 16 : s1 // 16]))

        def round_and_quantise(a, t0, n, on_scalar):
            grouped = held.tile([P, n, 4], BF16, name=f"grouped{a}_{t0}", tag={(2, 0): "late", (2, 512): "later"}.get((a, t0), f"grouped{a}_{t0}"), align_bytes=64)
            v = n - on_scalar
            if on_scalar:
                nc.scalar.activation(
                    out=grouped[:, v:n, :].rearrange("p (c i) j -> p c j i", i=4),
                    in_=raw[a, t0][:, :, v:n].rearrange("p j (c i) -> p c j i", i=4),
                    func=COPY,
                )
            if v:
                nc.vector.tensor_copy(
                    out=grouped[:, 0:v, :].rearrange("p (c i) j -> p c j i", i=4),
                    in_=raw[a, t0][:, :, 0:v].rearrange("p j (c i) -> p c j i", i=4),
                )
            for u0, u1 in ((0, v), (v, n)):
                if u0 < u1:
                    nc.vector.quantize_mx(
                        out=codes[a][:, t0 + u0 : t0 + u1].bitcast(FP8X4),
                        scales=planes[PLANE[a] : P, t0 + u0 : t0 + u1],
                        in_=grouped[:, u0:u1, :].rearrange("p t j -> p (t j)"),
                    )

        round_and_quantise(0, 0, 256, 0)
        round_and_quantise(0, 256, 256, 256)
        round_and_quantise(0, 512, 256, 0)
        round_and_quantise(0, 768, 256, 128)
        gather_codes(0, 0, 1536)
        gather_codes(0, 1536, 2688)
        round_and_quantise(1, 0, 512, 512)
        round_and_quantise(1, 512, 512, 512)
        gather_codes(0, 2688, 3072)
        gather_codes(1, 0, 1536)
        gather_codes(1, 1536, 2304)
        round_and_quantise(2, 0, 512, 512)
        round_and_quantise(2, 512, 512, 512)
        gates = held.tile([P, TOP, T], F32, name="gates", tag="late", align_bytes=64)
        nc.scalar.dma_start(out=gates[:], in_=gate.rearrange("r p t -> p r t"))

        def gather_bytes(s0, s1):
            nc.vector.tensor_copy(out=slot_planes[:, s0:s1], in_=planes[:].indirect(offs_t[:, s0 // 16 : s1 // 16]))
            for q in range(4):
                nc.sync.dma_start(
                    out=low[32 * q : 32 * q + 4, s0:s1].bitcast(I32),
                    in_=slot_planes[32 * q + 8 : 32 * q + 12, s0:s1].bitcast(I32),
                )

        gather_bytes(0, 768)
        gather_codes(2, 0, 768)
        gather_bytes(768, 2304)
        gather_codes(2, 768, 1536)
        gather_bytes(2304, 3072)
        gather_codes(2, 1536, 2304)
        late_codes = held.tile([P, S - HELD_BACK], U32, name="late_codes", tag="later", align_bytes=64)
        nc.vector.tensor_copy(out=late_codes[:], in_=codes[1][:].indirect(offs_t[:, HELD_BACK // 16 : S // 16]))
        gather_codes(2, 2304, 2816)
        gather_codes(2, 2816, 2944)
        gather_codes(2, 2944, 3072)

        y = held.tile([P, S], F32, name="y")
        for s0 in range(0, S, 128):
            e = s0 // C
            cols = slice(s0, s0 + 128)
            acc = psum.tile([P, 128], F32, name="acc")
            for a in range(PASSES):
                if a == 0:
                    lhsT, lhsT_scale = w8[:, e, :].bitcast(FP8X4), ws8[:, e, :]
                else:
                    m = 2 * e + a - 1
                    lhsT, lhsT_scale = w4[:, m, :].bitcast(FP4X4), ws4[:, m, :]
                nc.tensor.matmul_mx(
                    out=acc[:],
                    lhsT=lhsT,
                    lhsT_scale=lhsT_scale,
                    rhs=(
                        late_codes[:, s0 - HELD_BACK : s0 - HELD_BACK + 128]
                        if a == 1 and s0 >= HELD_BACK
                        else slot_codes[a][:, cols]
                    ).bitcast(FP8X4),
                    rhs_scale=low[:, cols] if a == 2 else slot_planes[PLANE[a] : P, cols],
                    start=(a == 0),
                    stop=(a == PASSES - 1),
                )
            nc.scalar.activation(out=y[:, cols], in_=acc[:], func=SILU, bias=bias[:, e : e + 1])

        parts = [held.tile([P, T], F32, name=f"part{r}") for r in range(TOP)]
        total = held.tile([P, T], F32, name="total")
        result = held.tile([P, T], F32, name="result")

        def fetch(r, t0, t1):
            nc.vector.tensor_tensor(
                parts[r][:, t0:t1], y[:].indirect(pos_t[r][:, t0 // 16 : t1 // 16]), gates[:, r, t0:t1], MULT
            )

        def finish(t0, t1):
            nc.vector.tensor_add(result[:, t0:t1], total[:, t0:t1], parts[2][:, t0:t1])
            nc.sync.dma_start(out=out[:, t0:t1], in_=result[:, t0:t1])

        fetch(0, 0, T)
        fetch(1, 0, T)
        fetch(2, 0, 512)
        nc.vector.tensor_add(total[:], parts[0][:], parts[1][:])
        fetch(2, 512, 768)
        finish(0, 512)
        fetch(2, 768, T)
        finish(512, 768)
        finish(768, T)
